import numpy as np
import ml_dtypes


def mxq(x, axis, fmt="e4m3"):
    dtype, down = {"e4m3": (ml_dtypes.float8_e4m3fn, 7), "e5m2": (ml_dtypes.float8_e5m2, 14)}[fmt]
    v = np.moveaxis(np.asarray(x, np.float32).astype(ml_dtypes.bfloat16).astype(np.float64), axis, -1)
    blocks = v.reshape(v.shape[:-1] + (-1, 32))
    amax = np.abs(blocks).max(-1, keepdims=True)
    byte = np.maximum(np.where(amax > 0, np.frexp(amax)[1] - 1 + 127, 0) - down, 1)
    scale = np.exp2(byte - 127.0)
    codes = (blocks / scale).astype(np.float32).astype(dtype).astype(np.float64)
    return np.moveaxis((codes * scale).reshape(v.shape), -1, axis)


WIDE = False


def mx_kscale(k):
    if not WIDE:
        return np.ones(k)
    levels = np.array([10, -10, 5, -5, 0])
    if k % 512:
        return np.exp2(np.random.permutation(np.resize(levels, k // 32))).repeat(32)
    a = np.empty((k // 512, 16))
    for p in range(k // 512):
        a[p, :8] = np.random.permutation(np.resize(levels, 8))
        for g in range(8):
            far = levels[np.abs(levels - a[p, g]) >= 10]
            a[p, g + 8] = far[np.random.randint(len(far))]
    return np.exp2(a.ravel()).repeat(32)


def f64(x):
    return np.asarray(x).astype(np.float64)


def striped(idx):
    return np.tile(idx.reshape(-1, 16).T, (8, 1)).astype(np.uint16)


def unstriped(offs):
    return offs[:16].T.reshape(-1).astype(np.int64)


def striped8(idx):
    return np.concatenate([x.reshape(-1, 16).T for x in idx]).astype(np.uint16)


def runs(offs, k):
    lists = np.stack([offs[16 * r : 16 * r + 16].T.reshape(-1) for r in range(8)]).astype(np.int64)
    return lists[np.arange(k) % 512 // 64]


def pack_weight(w):
    k, n = w.shape
    w = f64(np.asarray(w, np.float32).astype(ml_dtypes.bfloat16)).reshape(k // 32, 32, n)
    amax = np.abs(w).max(1)
    byte = np.clip(np.where(amax > 0, np.frexp(amax)[1] - 1 + 127 - 7, 1), 1, 254)
    scaled = (w * np.exp2(127.0 - byte)[:, None, :]).reshape(k, n).astype(np.float32)
    words = np.ascontiguousarray(scaled.reshape(k // 512, 128, 4, n).transpose(0, 1, 3, 2)).astype(ml_dtypes.float8_e4m3fn).view(np.uint8)
    return words, np.ascontiguousarray(byte.astype(np.uint8).reshape(k // 512, 16, n))


def unpack_weight(words, scales):
    g, p, n, _ = words.shape
    vals = np.ascontiguousarray(words).view(ml_dtypes.float8_e4m3fn).astype(np.float64) * np.repeat(np.exp2(scales.astype(np.float64) - 127.0), 8, axis=1)[..., None]
    return vals.transpose(0, 1, 3, 2).reshape(g * 512, n)


E2M1 = np.array([0.0, 0.5, 1.0, 1.5, 2.0, 3.0, 4.0, 6.0, -0.0, -0.5, -1.0, -1.5, -2.0, -3.0, -4.0, -6.0])


def pack_fp4(w):
    k, n = w.shape
    w = f64(np.asarray(w, np.float32).astype(ml_dtypes.bfloat16)).reshape(k // 32, 32, n)
    amax = np.abs(w).max(1)
    mant, ex = np.frexp(amax / 6.0)
    byte = np.clip(np.where(amax > 0, np.where(mant > 0.5, ex, ex - 1) + 127, 1), 1, 254)
    scaled = (w * np.exp2(127.0 - byte)[:, None, :]).reshape(k, n).astype(np.float32)
    c = np.ascontiguousarray(scaled.reshape(k // 512, 128, 4, n).transpose(0, 1, 3, 2)).astype(ml_dtypes.float4_e2m1fn).view(np.uint8) & 0xF
    words = (c[..., 0::2] | (c[..., 1::2] << 4)).reshape(k // 512, 128, 2 * n)
    return np.ascontiguousarray(words), np.ascontiguousarray(byte.astype(np.uint8).reshape(k // 512, 16, n))


def unpack_fp4(words, scales):
    g, _, n = scales.shape
    words = np.ascontiguousarray(words).reshape(g, 128, n, 2)
    nib = np.empty((g, 128, n, 4), np.uint8)
    nib[..., 0::2] = words & 0xF
    nib[..., 1::2] = words >> 4
    vals = E2M1[nib] * np.repeat(np.exp2(scales.astype(np.float64) - 127.0), 8, axis=1)[..., None]
    return vals.transpose(0, 1, 3, 2).reshape(g * 512, n)


def planes(y):
    n, m = y.shape
    v = y.astype(np.float32).astype(ml_dtypes.bfloat16).astype(np.float64).reshape(n // 32, 32, m)
    top = np.abs(v).max(1)
    byte = np.clip(np.where(top > 0, np.frexp(top)[1] - 1 + 127 - 7, 1), 1, 254)
    codes = (v * np.exp2(127.0 - byte)[:, None, :]).reshape(n, m).astype(np.float32).astype(ml_dtypes.float8_e4m3fn).view(np.uint8)
    words = codes.reshape(n // 512, 128, 4, m).transpose(0, 1, 3, 2)
    return np.ascontiguousarray(words), np.ascontiguousarray(byte.astype(np.uint8).reshape(n // 512, 16, m))


K, T, S, H, G, W = 512, 1024, 512, 512, 2048, 256


def setup_inputs():
    n = np.random.standard_normal
    s = mx_kscale(K)[:, None]
    packed_xT = pack_weight(n((K, T)) * s)
    packed_w1 = pack_fp4(n((K, H)) / np.sqrt(K) / s)
    packed_w2 = pack_fp4(n((K, H)) / np.sqrt(K) / s)
    packed_dT = pack_weight(n((K, G)) / s)
    perm = np.stack([np.random.permutation(S) for _ in range(8)])
    return {
        "x_words": packed_xT[0],
        "x_scales": packed_xT[1],
        "w1_words": packed_w1[0],
        "w1_scales": packed_w1[1],
        "w2_words": packed_w2[0],
        "w2_scales": packed_w2[1],
        "gs": (np.random.uniform(0.5, 1.5, (K, 1)) * s).astype(np.float32),
        "d_words": packed_dT[0],
        "d_scales": packed_dT[1],
        "offs": striped(np.random.permutation(T)[:S]),
        "two": striped(np.random.permutation(T)[:S]),
        "n1": striped8(np.stack([np.random.permutation(S) for _ in range(8)])),
        "n2": striped8(np.stack([np.random.permutation(S) for _ in range(8)])),
        "k1": striped8(np.random.randint(0, G, (8, H))),
        "n3": striped8(perm[:, :W]),
        "n4": striped8(perm[:, W:]),
    }


def reference(x_words, x_scales, w1_words, w1_scales, w2_words, w2_scales, gs, d_words, d_scales, offs, two, n1, n2, k1, n3, n4):
    d_k1 = unpack_weight(d_words, d_scales)[np.arange(K)[:, None], runs(k1, K)]
    xq = unpack_weight(x_words, x_scales)[:, unstriped(offs)]
    y = unpack_fp4(w1_words, w1_scales).T @ xq
    x_two = unpack_weight(x_words, x_scales)[:, unstriped(two)]
    d = unpack_fp4(w2_words, w2_scales).T @ x_two
    z = f64(gs) * (y * (np.tanh(d[np.arange(H)[:, None], runs(n1, H)] - (d[np.arange(H)[:, None], runs(n2, H)]))))
    h = 0.0625 * ((d_k1.T @ mxq(z, 0, "e4m3")))
    pb = h[np.arange(H)[:, None], runs(n4, H)]
    pa = h[np.arange(H)[:, None], runs(n3, H)]
    rb = pb - (0.5 * pa)
    ra = np.sqrt((pa) ** 2 + (pb) ** 2 + 0.25)
    ds = np.zeros((H, S))
    ds[np.arange(H)[:, None], runs(n3, H)] = ra
    out = ds.copy()
    out[np.arange(H)[:, None], runs(n4, H)] = rb
    return (out,) + planes(out)

@@ -1,0 +1,267 @@
+from contextlib import ExitStack
+
+import concourse.mybir as mybir
+from concourse.masks import make_identity
+
+K, T, S, H, G, W = 512, 1024, 512, 512, 2048, 256
+FLOPS = 3 * 2 * K * H * S
+
+F32 = mybir.dt.float32
+BF16 = mybir.dt.bfloat16
+I32 = mybir.dt.int32
+U32 = mybir.dt.uint32
+U16 = mybir.dt.uint16
+U8 = mybir.dt.uint8
+FP8X4 = mybir.dt.float8_e4m3fn_x4
+FP4X4 = mybir.dt.float4_e2m1fn_x4
+ACT = mybir.ActivationFunctionType
+ALU = mybir.AluOpType
+
+P = 128
+PACK = 4
+HALF = S // 2
+BOTH_ON_SCALAR = (0, 1, 5)
+LAG = 2
+
+
+def tile_picked_twqjointbpolar_none_po_kernel(
+    tc, x_words, x_scales, w1_words, w1_scales, w2_words, w2_scales, gs, d_words, d_scales,
+    offs, two, n1, n2, k1, n3, n4, out_0, out_1, out_2,
+):
+    nc = tc.nc
+    with ExitStack() as ctx:
+        keep = ctx.enter_context(tc.tile_pool(name="keep", bufs=1))
+        psum = ctx.enter_context(tc.psum_pool(name="psum", bufs=1))
+
+        def sb(name, shape, dtype, tag=None):
+            return keep.tile(shape, dtype, name=name, tag=tag or name, align_bytes=64)
+
+        def load_list(name, src):
+            tile = keep.tile(list(src.shape), U16, name=name)
+            nc.sync.dma_start(tile[:], src)
+            return tile
+
+        def load_scale_rows(queue, tile, src, repeats):
+            rows = src[0].bitcast(I32)
+            for q in range(4):
+                four = rows[4 * q : 4 * q + 4, :]
+                queue.dma_start(
+                    tile[32 * q : 32 * q + 4 * repeats, :].bitcast(I32),
+                    four.partition_broadcast(repeats) if repeats > 1 else four,
+                )
+
+        def cols(lst, start, count):
+            return lst[:, start // 16 : (start + count) // 16]
+
+        x_tab = sb("x_tab", [P, T], U32)
+        xs_tab = sb("xs_tab", [P, T], U8)
+        w_raw = [sb("w_raw%d" % i, [P, 2 * H], U8) for i in range(2)]
+        ws_raw = [sb("ws_raw%d" % i, [P, H], U8) for i in range(2)]
+        d_tab = sb("d_tab", [P, G], U32)
+        ds_tab = sb("ds_tab", [P, G], U8)
+        dk_scales = sb("dk_scales", [P, H], U8)
+        gs_t = sb("gs_t", [P, PACK], F32)
+        quarter = sb("quarter", [P, 1], F32)
+
+        ident = sb("ident", [P, P], F32)
+
+        nc.gpsimd.memset(ds_tab[:].bitcast(I32), 0)
+        nc.gpsimd.memset(ws_raw[0][:].bitcast(I32), 0)
+        nc.gpsimd.memset(dk_scales[:].bitcast(I32), 0)
+        nc.gpsimd.memset(quarter[:], 0.25)
+        make_identity(nc, ident[:])
+
+        two_t = load_list("two_t", two)
+        nc.sync.dma_start(x_tab[:].bitcast(I32), x_words[0].rearrange("p c r -> p (c r)").bitcast(I32))
+        load_scale_rows(nc.scalar, xs_tab, x_scales, 8)
+        nc.sync.dma_start(w_raw[1][:].bitcast(I32), w2_words[0].bitcast(I32))
+        load_scale_rows(nc.sync, ws_raw[1], w2_scales, 8)
+        offs_t = load_list("offs_t", offs)
+        n2_t = load_list("n2_t", n2)
+        n1_t = load_list("n1_t", n1)
+        k1_t = load_list("k1_t", k1)
+        nc.sync.dma_start(d_tab[:].bitcast(I32), d_words[0].rearrange("p c r -> p (c r)").bitcast(I32))
+        nc.sync.dma_start(ds_tab[0:P:8, :].bitcast(I32), d_scales[0].bitcast(I32))
+        nc.sync.dma_start(w_raw[0][:].bitcast(I32), w1_words[0].bitcast(I32))
+        load_scale_rows(nc.sync, ws_raw[0], w1_scales, 1)
+        nc.sync.dma_start(gs_t[:], gs.rearrange("(p t) o -> p (t o)", t=PACK))
+        n3_t = load_list("n3_t", n3)
+        n4_t = load_list("n4_t", n4)
+
+        def first_product(i, lst, tag):
+            w_dealt = sb("w_dealt%d" % i, [P, 2 * H], U8)
+            ws_dealt = sb("ws_dealt%d" % i, [P, H], U8)
+            nc.scalar.copy(
+                out=w_dealt[:].bitcast(U16).rearrange("p (t m) -> p m t", t=PACK),
+                in_=w_raw[i][:].bitcast(U16).rearrange("p (m t) -> p m t", t=PACK),
+            )
+            nc.gpsimd.tensor_copy(
+                out=ws_dealt[:].rearrange("p (t m) -> p t m", t=PACK),
+                in_=ws_raw[i][:].rearrange("p (m t) -> p t m", t=PACK),
+            )
+            xg = sb("xg%d" % i, [P, S], U32)
+            xsg = sb("xsg%d" % i, [P, S], U8)
+            nc.vector.tensor_copy(xsg[:], xs_tab[:].indirect(lst[:]))
+            nc.vector.tensor_copy(xg[:], x_tab[:].indirect(lst[:]))
+            banks = []
+            for t in range(PACK):
+                bank = psum.tile([P, S], F32, name="%s%d" % (tag, t), tag="%s%d" % (tag, t))
+                nc.tensor.matmul_mx(
+                    out=bank[:],
+                    lhsT=w_dealt[:, 2 * P * t : 2 * P * (t + 1)].bitcast(FP4X4),
+                    lhsT_scale=ws_dealt[:, P * t : P * (t + 1)],
+                    rhs=xg[:].bitcast(FP8X4),
+                    rhs_scale=xsg[:],
+                    start=True,
+                    stop=True,
+                )
+                banks.append(bank)
+            return banks
+
+        d_ps = first_product(1, two_t, "a")
+        d_sb = [sb("d_sb%d" % t, [P, S], F32) for t in range(PACK)]
+        y_ps = first_product(0, offs_t, "b")
+
+        dkg = sb("dkg", [P, H], U32)
+        dksg = sb("dksg", [P, H], U8)
+        dk_words = sb("dk_words", [P, H], U32)
+        dks_dealt = sb("dks_dealt", [P, H], U8)
+        nc.vector.tensor_copy(dksg[:], ds_tab[:].indirect(k1_t[:]))
+        nc.vector.tensor_copy(
+            out=dks_dealt[:].rearrange("p (t m) -> p m t", t=PACK),
+            in_=dksg[:].rearrange("p (m t) -> p m t", t=PACK),
+        )
+        for r in range(4):
+            nc.sync.dma_start(dk_scales[r:P:32, :].bitcast(I32), dks_dealt[8 * r : P : 32, :].bitcast(I32))
+        nc.vector.tensor_copy(dkg[:], d_tab[:].indirect(k1_t[:]))
+        nc.vector.tensor_copy(
+            out=dk_words[:].rearrange("p (t m) -> p m t", t=PACK),
+            in_=dkg[:].rearrange("p (m t) -> p m t", t=PACK),
+        )
+
+        h_ps = [psum.tile([P, S], F32, name="h%d" % t, tag="a%d" % t) for t in range(PACK)]
+        h_sb = [sb("h_sb%d" % t, [P, S], F32) for t in range(PACK)]
+        z_planes = [sb("z_planes%d" % hf, [P, PACK, HALF], BF16) for hf in range(2)]
+        diffs = {}
+
+        def fetch(u):
+            hf, t = divmod(u, PACK)
+            if hf == 0:
+                nc.scalar.activation(d_sb[t][:], d_ps[t][:], ACT.Copy)
+            g2 = sb("g2_%d" % u, [P, HALF], F32)
+            diff = sb("diff%d" % u, [P, HALF], F32, tag="dkg" if u == 0 else None)
+            nc.scalar.activation(g2[:], d_sb[t][:].indirect(cols(n2_t, hf * HALF, HALF)), ACT.Copy)
+            if u in BOTH_ON_SCALAR:
+                g1 = sb("g1_%d" % u, [P, HALF], F32)
+                nc.scalar.activation(g1[:], d_sb[t][:].indirect(cols(n1_t, hf * HALF, HALF)), ACT.Copy)
+                nc.vector.tensor_tensor(diff[:], g1[:], g2[:], ALU.subtract)
+            else:
+                nc.vector.tensor_tensor(diff[:], d_sb[t][:].indirect(cols(n1_t, hf * HALF, HALF)), g2[:], ALU.subtract)
+            diffs[u] = diff
+
+        def join(u):
+            hf, t = divmod(u, PACK)
+            th = sb("th%d" % u, [P, HALF], F32)
+            nc.scalar.activation(th[:], diffs[u][:], ACT.Tanh)
+            nc.vector.scalar_tensor_tensor(
+                out=z_planes[hf][:, t, :], in0=y_ps[t][:, hf * HALF : (hf + 1) * HALF], scalar=gs_t[:, t : t + 1],
+                in1=th[:], op0=ALU.mult, op1=ALU.mult,
+            )
+
+        def regroup(engine_copy, grouped, planes):
+            engine_copy(
+                out=grouped.rearrange("p (c i t) -> p c t i", i=4, t=PACK),
+                in_=planes.rearrange("p t (c i) -> p c t i", i=4),
+            )
+
+        def coded_product(hf):
+            z_grouped = sb("z_grouped%d" % hf, [P, HALF * PACK], BF16)
+            z_words = sb("z_words%d" % hf, [P, HALF], U32)
+            z_scales = sb("z_scales%d" % hf, [P, HALF], U8)
+            regroup(nc.vector.tensor_copy, z_grouped[:], z_planes[hf][:])
+            nc.vector.quantize_mx(out=z_words[:].bitcast(FP8X4), scales=z_scales[:], in_=z_grouped[:])
+            for t in range(PACK):
+                nc.tensor.matmul_mx(
+                    out=h_ps[t][:, hf * HALF : (hf + 1) * HALF],
+                    lhsT=dk_words[:, P * t : P * (t + 1)].bitcast(FP8X4),
+                    lhsT_scale=dk_scales[:, P * t : P * (t + 1)],
+                    rhs=z_words[:].bitcast(FP8X4),
+                    rhs_scale=z_scales[:],
+                    start=True,
+                    stop=True,
+                )
+
+        def leave_bank(t, hf):
+            js = slice(hf * HALF, (hf + 1) * HALF)
+            nc.scalar.activation(h_sb[t][:, js], h_ps[t][:, js], ACT.Copy, scale=0.0625)
+
+        units = 2 * PACK
+        for step in range(units + LAG):
+            if step < units:
+                fetch(step)
+            if step == units:
+                for t in range(PACK):
+                    leave_bank(t, 0)
+            if step >= LAG:
+                join(step - LAG)
+                if (step - LAG) % PACK == PACK - 1:
+                    coded_product((step - LAG) // PACK)
+
+        out_rows = out_0.rearrange("(p t) c -> p t c", t=PACK)
+        o_planes = sb("o_planes", [P, PACK, S], F32)
+        o_sb = [sb("o%d" % t, [P, S], F32) for t in range(PACK)]
+        turned = {}
+
+        def pick_pairs(t):
+            leave_bank(t, 1)
+            pair = sb("pair%d" % t, [P, 2 * W], F32)
+            nc.scalar.activation(pair[:, :W], h_sb[t][:].indirect(n3_t[:]), ACT.Copy, scale=-0.5)
+            if t == 0:
+                nc.vector.tensor_copy(pair[:, W:], h_sb[t][:].indirect(n4_t[:]))
+            else:
+                nc.scalar.activation(pair[:, W:], h_sb[t][:].indirect(n4_t[:]), ACT.Copy)
+            nc.vector.tensor_tensor(o_sb[t][:].indirect(n4_t[:]), pair[:, :W], pair[:, W:], ALU.add)
+            turned[t] = psum.tile([P, 2 * W], F32, name="turned%d" % t, tag="b%d" % (t % 2))
+            for b in range(2 * W // P):
+                nc.tensor.transpose(turned[t][:, b * P : (b + 1) * P], pair[:, b * P : (b + 1) * P], ident[:])
+
+        def put_radius(t):
+            sq = sb("sq%d" % t, [P, 2 * W], F32)
+            ra = sb("ra%d" % t, [P, W], F32)
+            nc.scalar.activation(sq[:, :W], turned[t][:, :W], ACT.Square, scale=2.0)
+            nc.scalar.activation(sq[:, W:], turned[t][:, W:], ACT.Square)
+            ssum = psum.tile([P, W], F32, name="ssum%d" % t, tag="b%d" % (2 + t % 2))
+            for b in range(W // P):
+                for side in range(2):
+                    nc.tensor.matmul(
+                        ssum[:, b * P : (b + 1) * P], sq[:, side * W + b * P : side * W + (b + 1) * P], ident[:],
+                        start=side == 0, stop=side == 1, is_transpose=True,
+                    )
+            nc.scalar.activation(ra[:], ssum[:], ACT.Sqrt, bias=quarter[:])
+            nc.vector.tensor_copy(o_sb[t][:].indirect(n3_t[:]), ra[:])
+            nc.sync.dma_start(out_rows[:, t, :], o_sb[t][:])
+            if t < PACK - 2:
+                nc.sync.dma_start(o_planes[:, t, :], o_sb[t][:])
+            elif t == PACK - 2:
+                nc.scalar.copy(o_planes[:, t, :], o_sb[t][:])
+
+        for step in range(PACK + 1):
+            if step < PACK:
+                pick_pairs(step)
+            if step >= 1:
+                put_radius(step - 1)
+
+        o_scales = sb("o_scales", [P, S], U8)
+        words_out = out_1[0].rearrange("p c r -> p (c r)").bitcast(I32)
+        for hf, engine_copy in enumerate((nc.vector.tensor_copy, nc.scalar.copy)):
+            js = slice(hf * HALF, (hf + 1) * HALF)
+            o_grouped = sb("o_grouped%d" % hf, [P, HALF * PACK], BF16)
+            o_words = sb("o_words%d" % hf, [P, HALF], U32)
+            engine_copy(o_planes[:, PACK - 1, js], o_sb[PACK - 1][:, js])
+            regroup(engine_copy, o_grouped[:], o_planes[:, :, js])
+            nc.vector.quantize_mx(out=o_words[:].bitcast(FP8X4), scales=o_scales[:, js], in_=o_grouped[:])
+            nc.sync.dma_start(words_out[:, js], o_words[:].bitcast(I32))
+        scale_rows = out_2[0].bitcast(I32)
+        for q in range(4):
+            queue = nc.scalar if q % 2 else nc.sync
+            queue.dma_start(scale_rows[4 * q : 4 * q + 4, :], o_scales[32 * q : 32 * q + 4, :].bitcast(I32))

@@ -20,7 +20,8 @@ ALU = mybir.AluOpType
 P = 128
 PACK = 4
 HALF = S // 2
-BOTH_ON_SCALAR = (0, 1, 5)
+BOTH_ON_SCALAR = (0, 1, 7)
+EARLY = 2
 LAG = 2
 
 
@@ -33,8 +34,8 @@ def tile_picked_twqjointbpolar_none_po_kernel(
         keep = ctx.enter_context(tc.tile_pool(name="keep", bufs=1))
         psum = ctx.enter_context(tc.psum_pool(name="psum", bufs=1))
 
-        def sb(name, shape, dtype, tag=None):
-            return keep.tile(shape, dtype, name=name, tag=tag or name, align_bytes=64)
+        def sb(name, shape, dtype, tag=None, bufs=1):
+            return keep.tile(shape, dtype, name=name, tag=tag or name, bufs=bufs, align_bytes=64)
 
         def load_list(name, src):
             tile = keep.tile(list(src.shape), U16, name=name)
@@ -76,13 +77,13 @@ def tile_picked_twqjointbpolar_none_po_kernel(
         load_scale_rows(nc.scalar, xs_tab, x_scales, 8)
         nc.sync.dma_start(w_raw[1][:].bitcast(I32), w2_words[0].bitcast(I32))
         load_scale_rows(nc.sync, ws_raw[1], w2_scales, 8)
+        nc.sync.dma_start(w_raw[0][:].bitcast(I32), w1_words[0].bitcast(I32))
         offs_t = load_list("offs_t", offs)
         n2_t = load_list("n2_t", n2)
         n1_t = load_list("n1_t", n1)
-        k1_t = load_list("k1_t", k1)
         nc.sync.dma_start(d_tab[:].bitcast(I32), d_words[0].rearrange("p c r -> p (c r)").bitcast(I32))
+        k1_t = load_list("k1_t", k1)
         nc.sync.dma_start(ds_tab[0:P:8, :].bitcast(I32), d_scales[0].bitcast(I32))
-        nc.sync.dma_start(w_raw[0][:].bitcast(I32), w1_words[0].bitcast(I32))
         load_scale_rows(nc.sync, ws_raw[0], w1_scales, 1)
         nc.sync.dma_start(gs_t[:], gs.rearrange("(p t) o -> p (t o)", t=PACK))
         n3_t = load_list("n3_t", n3)
@@ -95,9 +96,9 @@ def tile_picked_twqjointbpolar_none_po_kernel(
                 out=w_dealt[:].bitcast(U16).rearrange("p (t m) -> p m t", t=PACK),
                 in_=w_raw[i][:].bitcast(U16).rearrange("p (m t) -> p m t", t=PACK),
             )
-            nc.gpsimd.tensor_copy(
-                out=ws_dealt[:].rearrange("p (t m) -> p t m", t=PACK),
-                in_=ws_raw[i][:].rearrange("p (m t) -> p t m", t=PACK),
+            nc.vector.tensor_copy(
+                out=ws_dealt[:].rearrange("p (t m) -> p m t", t=PACK),
+                in_=ws_raw[i][:].rearrange("p (m t) -> p m t", t=PACK),
             )
             xg = sb("xg%d" % i, [P, S], U32)
             xsg = sb("xsg%d" % i, [P, S], U8)
@@ -142,27 +143,26 @@ def tile_picked_twqjointbpolar_none_po_kernel(
         h_ps = [psum.tile([P, S], F32, name="h%d" % t, tag="a%d" % t) for t in range(PACK)]
         h_sb = [sb("h_sb%d" % t, [P, S], F32) for t in range(PACK)]
         z_planes = [sb("z_planes%d" % hf, [P, PACK, HALF], BF16) for hf in range(2)]
-        diffs = {}
+        diffs = sb("diffs", [P, 2 * PACK, HALF], F32, tag="ws_raw0")
 
         def fetch(u):
             hf, t = divmod(u, PACK)
             if hf == 0:
                 nc.scalar.activation(d_sb[t][:], d_ps[t][:], ACT.Copy)
-            g2 = sb("g2_%d" % u, [P, HALF], F32)
-            diff = sb("diff%d" % u, [P, HALF], F32, tag="dkg" if u == 0 else None)
+            g2 = sb("g2_%d" % u, [P, HALF], F32, tag="g2", bufs=4)
+            diff = diffs[:, u, :]
             nc.scalar.activation(g2[:], d_sb[t][:].indirect(cols(n2_t, hf * HALF, HALF)), ACT.Copy)
             if u in BOTH_ON_SCALAR:
-                g1 = sb("g1_%d" % u, [P, HALF], F32)
+                g1 = sb("g1_%d" % u, [P, HALF], F32, tag="g1", bufs=2)
                 nc.scalar.activation(g1[:], d_sb[t][:].indirect(cols(n1_t, hf * HALF, HALF)), ACT.Copy)
-                nc.vector.tensor_tensor(diff[:], g1[:], g2[:], ALU.subtract)
+                nc.vector.tensor_tensor(diff, g1[:], g2[:], ALU.subtract)
             else:
-                nc.vector.tensor_tensor(diff[:], d_sb[t][:].indirect(cols(n1_t, hf * HALF, HALF)), g2[:], ALU.subtract)
-            diffs[u] = diff
+                nc.vector.tensor_tensor(diff, d_sb[t][:].indirect(cols(n1_t, hf * HALF, HALF)), g2[:], ALU.subtract)
 
         def join(u):
             hf, t = divmod(u, PACK)
             th = sb("th%d" % u, [P, HALF], F32)
-            nc.scalar.activation(th[:], diffs[u][:], ACT.Tanh)
+            nc.scalar.activation(th[:], diffs[:, u, :], ACT.Tanh)
             nc.vector.scalar_tensor_tensor(
                 out=z_planes[hf][:, t, :], in0=y_ps[t][:, hf * HALF : (hf + 1) * HALF], scalar=gs_t[:, t : t + 1],
                 in1=th[:], op0=ALU.mult, op1=ALU.mult,
@@ -191,8 +191,7 @@ def tile_picked_twqjointbpolar_none_po_kernel(
                     stop=True,
                 )
 
-        def leave_bank(t, hf):
-            js = slice(hf * HALF, (hf + 1) * HALF)
+        def leave_bank(t, js):
             nc.scalar.activation(h_sb[t][:, js], h_ps[t][:, js], ACT.Copy, scale=0.0625)
 
         units = 2 * PACK
@@ -200,8 +199,8 @@ def tile_picked_twqjointbpolar_none_po_kernel(
             if step < units:
                 fetch(step)
             if step == units:
-                for t in range(PACK):
-                    leave_bank(t, 0)
+                for t in range(EARLY):
+                    leave_bank(t, slice(0, HALF))
             if step >= LAG:
                 join(step - LAG)
                 if (step - LAG) % PACK == PACK - 1:
@@ -213,7 +212,10 @@ def tile_picked_twqjointbpolar_none_po_kernel(
         turned = {}
 
         def pick_pairs(t):
-            leave_bank(t, 1)
+            if t == 0:
+                nc.vector.tensor_scalar(h_sb[t][:, HALF:], h_ps[t][:, HALF:], 0.0625, None, ALU.mult)
+            else:
+                leave_bank(t, slice(HALF if t < EARLY else 0, S))
             pair = sb("pair%d" % t, [P, 2 * W], F32)
             nc.scalar.activation(pair[:, :W], h_sb[t][:].indirect(n3_t[:]), ACT.Copy, scale=-0.5)
             if t == 0:
@@ -226,7 +228,7 @@ def tile_picked_twqjointbpolar_none_po_kernel(
                 nc.tensor.transpose(turned[t][:, b * P : (b + 1) * P], pair[:, b * P : (b + 1) * P], ident[:])
 
         def put_radius(t):
-            sq = sb("sq%d" % t, [P, 2 * W], F32)
+            sq = o_planes[:, PACK - 2, :] if t == PACK - 1 else sb("sq%d" % t, [P, 2 * W], F32)
             ra = sb("ra%d" % t, [P, W], F32)
             nc.scalar.activation(sq[:, :W], turned[t][:, :W], ACT.Square, scale=2.0)
             nc.scalar.activation(sq[:, W:], turned[t][:, W:], ACT.Square)
@@ -238,12 +240,12 @@ def tile_picked_twqjointbpolar_none_po_kernel(
                         start=side == 0, stop=side == 1, is_transpose=True,
                     )
             nc.scalar.activation(ra[:], ssum[:], ACT.Sqrt, bias=quarter[:])
+            if t == PACK - 1:
+                nc.scalar.copy(o_planes[:, t - 1, :], o_sb[t - 1][:])
             nc.vector.tensor_copy(o_sb[t][:].indirect(n3_t[:]), ra[:])
             nc.sync.dma_start(out_rows[:, t, :], o_sb[t][:])
             if t < PACK - 2:
                 nc.sync.dma_start(o_planes[:, t, :], o_sb[t][:])
-            elif t == PACK - 2:
-                nc.scalar.copy(o_planes[:, t, :], o_sb[t][:])
 
         for step in range(PACK + 1):
             if step < PACK:

@@ -22,6 +22,7 @@ PACK = 4
 HALF = S // 2
 BOTH_ON_SCALAR = (0, 1, 7)
 EARLY = 2
+TAIL_SPLIT = 320
 LAG = 2
 
 
@@ -42,9 +43,9 @@ def tile_picked_twqjointbpolar_none_po_kernel(
             nc.sync.dma_start(tile[:], src)
             return tile
 
-        def load_scale_rows(queue, tile, src, repeats):
+        def load_scale_rows(queues, tile, src, repeats):
             rows = src[0].bitcast(I32)
-            for q in range(4):
+            for q, queue in enumerate(queues):
                 four = rows[4 * q : 4 * q + 4, :]
                 queue.dma_start(
                     tile[32 * q : 32 * q + 4 * repeats, :].bitcast(I32),
@@ -66,25 +67,25 @@ def tile_picked_twqjointbpolar_none_po_kernel(
 
         ident = sb("ident", [P, P], F32)
 
-        nc.gpsimd.memset(ds_tab[:].bitcast(I32), 0)
+        nc.vector.memset(ds_tab[:].bitcast(I32), 0)
         nc.gpsimd.memset(ws_raw[0][:].bitcast(I32), 0)
+        load_scale_rows([nc.gpsimd] * 4, ws_raw[0], w1_scales, 1)
         nc.gpsimd.memset(dk_scales[:].bitcast(I32), 0)
         nc.gpsimd.memset(quarter[:], 0.25)
         make_identity(nc, ident[:])
 
         two_t = load_list("two_t", two)
+        load_scale_rows([nc.sync] * 2 + [nc.scalar] * 2, xs_tab, x_scales, 8)
         nc.sync.dma_start(x_tab[:].bitcast(I32), x_words[0].rearrange("p c r -> p (c r)").bitcast(I32))
-        load_scale_rows(nc.scalar, xs_tab, x_scales, 8)
         nc.sync.dma_start(w_raw[1][:].bitcast(I32), w2_words[0].bitcast(I32))
-        load_scale_rows(nc.sync, ws_raw[1], w2_scales, 8)
+        load_scale_rows([nc.sync] * 4, ws_raw[1], w2_scales, 8)
         nc.sync.dma_start(w_raw[0][:].bitcast(I32), w1_words[0].bitcast(I32))
         offs_t = load_list("offs_t", offs)
         n2_t = load_list("n2_t", n2)
         n1_t = load_list("n1_t", n1)
         nc.sync.dma_start(d_tab[:].bitcast(I32), d_words[0].rearrange("p c r -> p (c r)").bitcast(I32))
-        k1_t = load_list("k1_t", k1)
         nc.sync.dma_start(ds_tab[0:P:8, :].bitcast(I32), d_scales[0].bitcast(I32))
-        load_scale_rows(nc.sync, ws_raw[0], w1_scales, 1)
+        k1_t = load_list("k1_t", k1)
         nc.sync.dma_start(gs_t[:], gs.rearrange("(p t) o -> p (t o)", t=PACK))
         n3_t = load_list("n3_t", n3)
         n4_t = load_list("n4_t", n4)
@@ -96,10 +97,16 @@ def tile_picked_twqjointbpolar_none_po_kernel(
                 out=w_dealt[:].bitcast(U16).rearrange("p (t m) -> p m t", t=PACK),
                 in_=w_raw[i][:].bitcast(U16).rearrange("p (m t) -> p m t", t=PACK),
             )
-            nc.vector.tensor_copy(
-                out=ws_dealt[:].rearrange("p (t m) -> p m t", t=PACK),
-                in_=ws_raw[i][:].rearrange("p (m t) -> p m t", t=PACK),
-            )
+            if i == 1:
+                nc.vector.tensor_copy(
+                    out=ws_dealt[:].rearrange("p (t m) -> p m t", t=PACK),
+                    in_=ws_raw[i][:].rearrange("p (m t) -> p m t", t=PACK),
+                )
+            else:
+                nc.gpsimd.tensor_copy(
+                    out=ws_dealt[:].rearrange("p (t m) -> p t m", t=PACK),
+                    in_=ws_raw[i][:].rearrange("p (m t) -> p t m", t=PACK),
+                )
             xg = sb("xg%d" % i, [P, S], U32)
             xsg = sb("xsg%d" % i, [P, S], U8)
             nc.vector.tensor_copy(xsg[:], xs_tab[:].indirect(lst[:]))
@@ -143,7 +150,7 @@ def tile_picked_twqjointbpolar_none_po_kernel(
         h_ps = [psum.tile([P, S], F32, name="h%d" % t, tag="a%d" % t) for t in range(PACK)]
         h_sb = [sb("h_sb%d" % t, [P, S], F32) for t in range(PACK)]
         z_planes = [sb("z_planes%d" % hf, [P, PACK, HALF], BF16) for hf in range(2)]
-        diffs = sb("diffs", [P, 2 * PACK, HALF], F32, tag="ws_raw0")
+        diffs = sb("diffs", [P, 2 * PACK, HALF], F32, tag="dkg")
 
         def fetch(u):
             hf, t = divmod(u, PACK)
@@ -243,9 +250,9 @@ def tile_picked_twqjointbpolar_none_po_kernel(
             if t == PACK - 1:
                 nc.scalar.copy(o_planes[:, t - 1, :], o_sb[t - 1][:])
             nc.vector.tensor_copy(o_sb[t][:].indirect(n3_t[:]), ra[:])
-            nc.sync.dma_start(out_rows[:, t, :], o_sb[t][:])
             if t < PACK - 2:
                 nc.sync.dma_start(o_planes[:, t, :], o_sb[t][:])
+            nc.sync.dma_start(out_rows[:, t, :], o_sb[t][:])
 
         for step in range(PACK + 1):
             if step < PACK:
@@ -255,13 +262,16 @@ def tile_picked_twqjointbpolar_none_po_kernel(
 
         o_scales = sb("o_scales", [P, S], U8)
         words_out = out_1[0].rearrange("p c r -> p (c r)").bitcast(I32)
-        for hf, engine_copy in enumerate((nc.vector.tensor_copy, nc.scalar.copy)):
-            js = slice(hf * HALF, (hf + 1) * HALF)
-            o_grouped = sb("o_grouped%d" % hf, [P, HALF * PACK], BF16)
-            o_words = sb("o_words%d" % hf, [P, HALF], U32)
+        o_grouped = sb("o_grouped", [P, S * PACK], BF16)
+        for engine_copy, js in ((nc.vector.tensor_copy, slice(0, TAIL_SPLIT)), (nc.scalar.copy, slice(TAIL_SPLIT, S))):
             engine_copy(o_planes[:, PACK - 1, js], o_sb[PACK - 1][:, js])
-            regroup(engine_copy, o_grouped[:], o_planes[:, :, js])
-            nc.vector.quantize_mx(out=o_words[:].bitcast(FP8X4), scales=o_scales[:, js], in_=o_grouped[:])
+            regroup(engine_copy, o_grouped[:, js.start * PACK : js.stop * PACK], o_planes[:, :, js])
+        for hf in range(2):
+            js = slice(hf * HALF, (hf + 1) * HALF)
+            o_words = sb("o_words%d" % hf, [P, HALF], U32)
+            nc.vector.quantize_mx(
+                out=o_words[:].bitcast(FP8X4), scales=o_scales[:, js], in_=o_grouped[:, js.start * PACK : js.stop * PACK]
+            )
             nc.sync.dma_start(words_out[:, js], o_words[:].bitcast(I32))
         scale_rows = out_2[0].bitcast(I32)
         for q in range(4):

@@ -170,6 +170,9 @@ def tile_picked_twqjointbpolar_none_po_kernel(
             hf, t = divmod(u, PACK)
             th = sb("th%d" % u, [P, HALF], F32)
             nc.scalar.activation(th[:], diffs[:, u, :], ACT.Tanh)
+            if u == 2 * PACK - 1:
+                warm = sb("warm", [P, 1], F32)
+                nc.scalar.activation(warm[:], th[:, 0:1], ACT.Sqrt, bias=quarter[:], scale=0.0)
             nc.vector.scalar_tensor_tensor(
                 out=z_planes[hf][:, t, :], in0=y_ps[t][:, hf * HALF : (hf + 1) * HALF], scalar=gs_t[:, t : t + 1],
                 in1=th[:], op0=ALU.mult, op1=ALU.mult,

@@ -19,11 +19,18 @@ ALU = mybir.AluOpType
 
 P = 128
 PACK = 4
+QUADRANTS = 4
 HALF = S // 2
-BOTH_ON_SCALAR = (0, 1, 7)
-EARLY = 2
-TAIL_SPLIT = 320
+UNITS = 2 * PACK
+LAST_UNIT = UNITS - 1
+H_SCALE = 0.0625
+
+BOTH_ON_SCALAR = (0, 1, LAST_UNIT)
 LAG = 2
+N2_BUFS = 4
+N1_BUFS = 2
+EARLY_TILES = 2
+TAIL_SPLIT = 320
 
 
 def tile_picked_twqjointbpolar_none_po_kernel(
@@ -52,24 +59,37 @@ def tile_picked_twqjointbpolar_none_po_kernel(
                     four.partition_broadcast(repeats) if repeats > 1 else four,
                 )
 
-        def cols(lst, start, count):
+        def entries(lst, start, count):
             return lst[:, start // 16 : (start + count) // 16]
+
+        def deal(engine_copy, dealt, plain, walk="p m t"):
+            engine_copy(
+                out=dealt.rearrange("p (t m) -> " + walk, t=PACK), in_=plain.rearrange("p (m t) -> " + walk, t=PACK)
+            )
+
+        def regroup(engine_copy, grouped, tiles):
+            engine_copy(
+                out=grouped.rearrange("p (c i t) -> p c t i", i=4, t=PACK),
+                in_=tiles.rearrange("p t (c i) -> p c t i", i=4),
+            )
+
+        def pieces(width):
+            return [slice(c, c + width) for c in range(0, HALF, width)]
 
         x_tab = sb("x_tab", [P, T], U32)
         xs_tab = sb("xs_tab", [P, T], U8)
-        w_raw = [sb("w_raw%d" % i, [P, 2 * H], U8) for i in range(2)]
-        ws_raw = [sb("ws_raw%d" % i, [P, H], U8) for i in range(2)]
+        w1_raw, w2_raw = (sb("w%d_raw" % i, [P, 2 * H], U8) for i in (1, 2))
+        w1s_raw, w2s_raw = (sb("w%ds_raw" % i, [P, H], U8) for i in (1, 2))
         d_tab = sb("d_tab", [P, G], U32)
         ds_tab = sb("ds_tab", [P, G], U8)
         dk_scales = sb("dk_scales", [P, H], U8)
         gs_t = sb("gs_t", [P, PACK], F32)
         quarter = sb("quarter", [P, 1], F32)
-
         ident = sb("ident", [P, P], F32)
 
         nc.vector.memset(ds_tab[:].bitcast(I32), 0)
-        nc.gpsimd.memset(ws_raw[0][:].bitcast(I32), 0)
-        load_scale_rows([nc.gpsimd] * 4, ws_raw[0], w1_scales, 1)
+        nc.gpsimd.memset(w1s_raw[:].bitcast(I32), 0)
+        load_scale_rows([nc.gpsimd] * QUADRANTS, w1s_raw, w1_scales, 1)
         nc.gpsimd.memset(dk_scales[:].bitcast(I32), 0)
         nc.gpsimd.memset(quarter[:], 0.25)
         make_identity(nc, ident[:])
@@ -77,9 +97,9 @@ def tile_picked_twqjointbpolar_none_po_kernel(
         two_t = load_list("two_t", two)
         load_scale_rows([nc.sync] * 2 + [nc.scalar] * 2, xs_tab, x_scales, 8)
         nc.sync.dma_start(x_tab[:].bitcast(I32), x_words[0].rearrange("p c r -> p (c r)").bitcast(I32))
-        nc.sync.dma_start(w_raw[1][:].bitcast(I32), w2_words[0].bitcast(I32))
-        load_scale_rows([nc.sync] * 4, ws_raw[1], w2_scales, 8)
-        nc.sync.dma_start(w_raw[0][:].bitcast(I32), w1_words[0].bitcast(I32))
+        nc.sync.dma_start(w2_raw[:].bitcast(I32), w2_words[0].bitcast(I32))
+        load_scale_rows([nc.sync] * QUADRANTS, w2s_raw, w2_scales, 8)
+        nc.sync.dma_start(w1_raw[:].bitcast(I32), w1_words[0].bitcast(I32))
         offs_t = load_list("offs_t", offs)
         n2_t = load_list("n2_t", n2)
         n1_t = load_list("n1_t", n1)
@@ -90,142 +110,130 @@ def tile_picked_twqjointbpolar_none_po_kernel(
         n3_t = load_list("n3_t", n3)
         n4_t = load_list("n4_t", n4)
 
-        def first_product(i, lst, tag):
-            w_dealt = sb("w_dealt%d" % i, [P, 2 * H], U8)
-            ws_dealt = sb("ws_dealt%d" % i, [P, H], U8)
-            nc.scalar.copy(
-                out=w_dealt[:].bitcast(U16).rearrange("p (t m) -> p m t", t=PACK),
-                in_=w_raw[i][:].bitcast(U16).rearrange("p (m t) -> p m t", t=PACK),
-            )
-            if i == 1:
-                nc.vector.tensor_copy(
-                    out=ws_dealt[:].rearrange("p (t m) -> p m t", t=PACK),
-                    in_=ws_raw[i][:].rearrange("p (m t) -> p m t", t=PACK),
-                )
-            else:
-                nc.gpsimd.tensor_copy(
-                    out=ws_dealt[:].rearrange("p (t m) -> p t m", t=PACK),
-                    in_=ws_raw[i][:].rearrange("p (m t) -> p t m", t=PACK),
-                )
-            xg = sb("xg%d" % i, [P, S], U32)
-            xsg = sb("xsg%d" % i, [P, S], U8)
-            nc.vector.tensor_copy(xsg[:], xs_tab[:].indirect(lst[:]))
-            nc.vector.tensor_copy(xg[:], x_tab[:].indirect(lst[:]))
+        def token_product(name, w_raw, ws_raw, deal_scales, lst, bank_tag):
+            w_dealt = sb(name + "_w", [P, 2 * H], U8)
+            ws_dealt = sb(name + "_ws", [P, H], U8)
+            deal(nc.scalar.copy, w_dealt[:].bitcast(U16), w_raw[:].bitcast(U16))
+            deal_scales(ws_dealt[:], ws_raw[:])
+            x_picked = sb(name + "_x", [P, S], U32)
+            xs_picked = sb(name + "_xs", [P, S], U8)
+            nc.vector.tensor_copy(xs_picked[:], xs_tab[:].indirect(lst[:]))
+            nc.vector.tensor_copy(x_picked[:], x_tab[:].indirect(lst[:]))
             banks = []
             for t in range(PACK):
-                bank = psum.tile([P, S], F32, name="%s%d" % (tag, t), tag="%s%d" % (tag, t))
+                bank = psum.tile([P, S], F32, name="%s_ps%d" % (name, t), tag="%s%d" % (bank_tag, t))
                 nc.tensor.matmul_mx(
                     out=bank[:],
                     lhsT=w_dealt[:, 2 * P * t : 2 * P * (t + 1)].bitcast(FP4X4),
                     lhsT_scale=ws_dealt[:, P * t : P * (t + 1)],
-                    rhs=xg[:].bitcast(FP8X4),
-                    rhs_scale=xsg[:],
+                    rhs=x_picked[:].bitcast(FP8X4),
+                    rhs_scale=xs_picked[:],
                     start=True,
                     stop=True,
                 )
                 banks.append(bank)
             return banks
 
-        d_ps = first_product(1, two_t, "a")
+        d_ps = token_product(
+            "d", w2_raw, w2s_raw, lambda dealt, plain: deal(nc.vector.tensor_copy, dealt, plain), two_t, "low"
+        )
         d_sb = [sb("d_sb%d" % t, [P, S], F32) for t in range(PACK)]
-        y_ps = first_product(0, offs_t, "b")
+        y_ps = token_product(
+            "y", w1_raw, w1s_raw, lambda dealt, plain: deal(nc.gpsimd.tensor_copy, dealt, plain, "p t m"), offs_t, "high"
+        )
 
-        dkg = sb("dkg", [P, H], U32)
-        dksg = sb("dksg", [P, H], U8)
+        dk_picked = sb("dk_picked", [P, H], U32)
+        dks_picked = sb("dks_picked", [P, H], U8)
         dk_words = sb("dk_words", [P, H], U32)
         dks_dealt = sb("dks_dealt", [P, H], U8)
-        nc.vector.tensor_copy(dksg[:], ds_tab[:].indirect(k1_t[:]))
-        nc.vector.tensor_copy(
-            out=dks_dealt[:].rearrange("p (t m) -> p m t", t=PACK),
-            in_=dksg[:].rearrange("p (m t) -> p m t", t=PACK),
-        )
+        nc.vector.tensor_copy(dks_picked[:], ds_tab[:].indirect(k1_t[:]))
+        deal(nc.vector.tensor_copy, dks_dealt[:], dks_picked[:])
         for r in range(4):
             nc.sync.dma_start(dk_scales[r:P:32, :].bitcast(I32), dks_dealt[8 * r : P : 32, :].bitcast(I32))
-        nc.vector.tensor_copy(dkg[:], d_tab[:].indirect(k1_t[:]))
-        nc.vector.tensor_copy(
-            out=dk_words[:].rearrange("p (t m) -> p m t", t=PACK),
-            in_=dkg[:].rearrange("p (m t) -> p m t", t=PACK),
-        )
+        nc.vector.tensor_copy(dk_picked[:], d_tab[:].indirect(k1_t[:]))
+        deal(nc.vector.tensor_copy, dk_words[:], dk_picked[:])
 
-        h_ps = [psum.tile([P, S], F32, name="h%d" % t, tag="a%d" % t) for t in range(PACK)]
+        h_ps = [psum.tile([P, S], F32, name="h_ps%d" % t, tag="low%d" % t) for t in range(PACK)]
         h_sb = [sb("h_sb%d" % t, [P, S], F32) for t in range(PACK)]
-        z_planes = [sb("z_planes%d" % hf, [P, PACK, HALF], BF16) for hf in range(2)]
-        diffs = sb("diffs", [P, 2 * PACK, HALF], F32, tag="dkg")
+        z_tiles = [sb("z_tiles%d" % hf, [P, PACK, HALF], BF16) for hf in range(2)]
+        diffs = sb("diffs", [P, UNITS, HALF], F32, tag="dk_picked")
 
-        def fetch(u):
+        def look_up_d(u):
             hf, t = divmod(u, PACK)
             if hf == 0:
                 nc.scalar.activation(d_sb[t][:], d_ps[t][:], ACT.Copy)
-            g2 = sb("g2_%d" % u, [P, HALF], F32, tag="g2", bufs=4)
-            diff = diffs[:, u, :]
-            nc.scalar.activation(g2[:], d_sb[t][:].indirect(cols(n2_t, hf * HALF, HALF)), ACT.Copy)
+            at_n2 = sb("at_n2_%d" % u, [P, HALF], F32, tag="at_n2", bufs=N2_BUFS)
+            nc.scalar.activation(at_n2[:], d_sb[t][:].indirect(entries(n2_t, hf * HALF, HALF)), ACT.Copy)
+            window_n1 = d_sb[t][:].indirect(entries(n1_t, hf * HALF, HALF))
             if u in BOTH_ON_SCALAR:
-                g1 = sb("g1_%d" % u, [P, HALF], F32, tag="g1", bufs=2)
-                nc.scalar.activation(g1[:], d_sb[t][:].indirect(cols(n1_t, hf * HALF, HALF)), ACT.Copy)
-                nc.vector.tensor_tensor(diff, g1[:], g2[:], ALU.subtract)
+                at_n1 = sb("at_n1_%d" % u, [P, HALF], F32, tag="at_n1", bufs=N1_BUFS)
+                nc.scalar.activation(at_n1[:], window_n1, ACT.Copy)
+                nc.vector.tensor_tensor(diffs[:, u, :], at_n1[:], at_n2[:], ALU.subtract)
             else:
-                nc.vector.tensor_tensor(diff, d_sb[t][:].indirect(cols(n1_t, hf * HALF, HALF)), g2[:], ALU.subtract)
+                nc.vector.tensor_tensor(diffs[:, u, :], window_n1, at_n2[:], ALU.subtract)
 
-        def join(u):
+        def gate(u):
             hf, t = divmod(u, PACK)
             th = sb("th%d" % u, [P, HALF], F32)
             nc.scalar.activation(th[:], diffs[:, u, :], ACT.Tanh)
-            if u == 2 * PACK - 1:
+            if u == LAST_UNIT:
                 warm = sb("warm", [P, 1], F32)
                 nc.scalar.activation(warm[:], th[:, 0:1], ACT.Sqrt, bias=quarter[:], scale=0.0)
-            nc.vector.scalar_tensor_tensor(
-                out=z_planes[hf][:, t, :], in0=y_ps[t][:, hf * HALF : (hf + 1) * HALF], scalar=gs_t[:, t : t + 1],
-                in1=th[:], op0=ALU.mult, op1=ALU.mult,
-            )
-
-        def regroup(engine_copy, grouped, planes):
-            engine_copy(
-                out=grouped.rearrange("p (c i t) -> p c t i", i=4, t=PACK),
-                in_=planes.rearrange("p t (c i) -> p c t i", i=4),
-            )
+            y_half = y_ps[t][:, hf * HALF : (hf + 1) * HALF]
+            for js in pieces(HALF // 2 if u == LAST_UNIT else HALF):
+                nc.vector.scalar_tensor_tensor(
+                    out=z_tiles[hf][:, t, js], in0=y_half[:, js], scalar=gs_t[:, t : t + 1], in1=th[:, js],
+                    op0=ALU.mult, op1=ALU.mult,
+                )
 
         def coded_product(hf):
             z_grouped = sb("z_grouped%d" % hf, [P, HALF * PACK], BF16)
             z_words = sb("z_words%d" % hf, [P, HALF], U32)
             z_scales = sb("z_scales%d" % hf, [P, HALF], U8)
-            regroup(nc.vector.tensor_copy, z_grouped[:], z_planes[hf][:])
-            nc.vector.quantize_mx(out=z_words[:].bitcast(FP8X4), scales=z_scales[:], in_=z_grouped[:])
-            for t in range(PACK):
-                nc.tensor.matmul_mx(
-                    out=h_ps[t][:, hf * HALF : (hf + 1) * HALF],
-                    lhsT=dk_words[:, P * t : P * (t + 1)].bitcast(FP8X4),
-                    lhsT_scale=dk_scales[:, P * t : P * (t + 1)],
-                    rhs=z_words[:].bitcast(FP8X4),
-                    rhs_scale=z_scales[:],
-                    start=True,
-                    stop=True,
+            cut = pieces(HALF // 2 if hf == 1 else HALF)
+            for js in cut:
+                regroup(nc.vector.tensor_copy, z_grouped[:, js.start * PACK : js.stop * PACK], z_tiles[hf][:, :, js])
+            for js in cut:
+                nc.vector.quantize_mx(
+                    out=z_words[:, js].bitcast(FP8X4), scales=z_scales[:, js],
+                    in_=z_grouped[:, js.start * PACK : js.stop * PACK],
                 )
+            for t in range(PACK):
+                for js in cut if t == 0 else pieces(HALF):
+                    nc.tensor.matmul_mx(
+                        out=h_ps[t][:, hf * HALF + js.start : hf * HALF + js.stop],
+                        lhsT=dk_words[:, P * t : P * (t + 1)].bitcast(FP8X4),
+                        lhsT_scale=dk_scales[:, P * t : P * (t + 1)],
+                        rhs=z_words[:, js].bitcast(FP8X4),
+                        rhs_scale=z_scales[:, js],
+                        start=True,
+                        stop=True,
+                    )
 
-        def leave_bank(t, js):
-            nc.scalar.activation(h_sb[t][:, js], h_ps[t][:, js], ACT.Copy, scale=0.0625)
+        def h_out_of_psum(t, js):
+            nc.scalar.activation(h_sb[t][:, js], h_ps[t][:, js], ACT.Copy, scale=H_SCALE)
 
-        units = 2 * PACK
-        for step in range(units + LAG):
-            if step < units:
-                fetch(step)
-            if step == units:
-                for t in range(EARLY):
-                    leave_bank(t, slice(0, HALF))
+        for step in range(UNITS + LAG):
+            if step < UNITS:
+                look_up_d(step)
+            if step == UNITS:
+                for t in range(EARLY_TILES):
+                    h_out_of_psum(t, slice(0, HALF))
             if step >= LAG:
-                join(step - LAG)
+                gate(step - LAG)
                 if (step - LAG) % PACK == PACK - 1:
                     coded_product((step - LAG) // PACK)
 
         out_rows = out_0.rearrange("(p t) c -> p t c", t=PACK)
-        o_planes = sb("o_planes", [P, PACK, S], F32)
-        o_sb = [sb("o%d" % t, [P, S], F32) for t in range(PACK)]
+        o_tiles = sb("o_tiles", [P, PACK, S], F32)
+        o_sb = [sb("o_sb%d" % t, [P, S], F32) for t in range(PACK)]
         turned = {}
 
         def pick_pairs(t):
             if t == 0:
-                nc.vector.tensor_scalar(h_sb[t][:, HALF:], h_ps[t][:, HALF:], 0.0625, None, ALU.mult)
+                nc.vector.tensor_scalar(h_sb[t][:, HALF:], h_ps[t][:, HALF:], H_SCALE, None, ALU.mult)
             else:
-                leave_bank(t, slice(HALF if t < EARLY else 0, S))
+                h_out_of_psum(t, slice(HALF if t < EARLY_TILES else 0, S))
             pair = sb("pair%d" % t, [P, 2 * W], F32)
             nc.scalar.activation(pair[:, :W], h_sb[t][:].indirect(n3_t[:]), ACT.Copy, scale=-0.5)
             if t == 0:
@@ -233,42 +241,44 @@ def tile_picked_twqjointbpolar_none_po_kernel(
             else:
                 nc.scalar.activation(pair[:, W:], h_sb[t][:].indirect(n4_t[:]), ACT.Copy)
             nc.vector.tensor_tensor(o_sb[t][:].indirect(n4_t[:]), pair[:, :W], pair[:, W:], ALU.add)
-            turned[t] = psum.tile([P, 2 * W], F32, name="turned%d" % t, tag="b%d" % (t % 2))
+            turned[t] = psum.tile([P, 2 * W], F32, name="turned%d" % t, tag="high%d" % (t % 2))
             for b in range(2 * W // P):
                 nc.tensor.transpose(turned[t][:, b * P : (b + 1) * P], pair[:, b * P : (b + 1) * P], ident[:])
 
-        def put_radius(t):
-            sq = o_planes[:, PACK - 2, :] if t == PACK - 1 else sb("sq%d" % t, [P, 2 * W], F32)
+        def put_roots(t):
+            sq = o_tiles[:, PACK - 2, :] if t == PACK - 1 else sb("sq%d" % t, [P, 2 * W], F32)
             ra = sb("ra%d" % t, [P, W], F32)
             nc.scalar.activation(sq[:, :W], turned[t][:, :W], ACT.Square, scale=2.0)
             nc.scalar.activation(sq[:, W:], turned[t][:, W:], ACT.Square)
-            ssum = psum.tile([P, W], F32, name="ssum%d" % t, tag="b%d" % (2 + t % 2))
+            sq_sum = psum.tile([P, W], F32, name="sq_sum%d" % t, tag="high%d" % (2 + t % 2))
             for b in range(W // P):
                 for side in range(2):
                     nc.tensor.matmul(
-                        ssum[:, b * P : (b + 1) * P], sq[:, side * W + b * P : side * W + (b + 1) * P], ident[:],
+                        sq_sum[:, b * P : (b + 1) * P], sq[:, side * W + b * P : side * W + (b + 1) * P], ident[:],
                         start=side == 0, stop=side == 1, is_transpose=True,
                     )
-            nc.scalar.activation(ra[:], ssum[:], ACT.Sqrt, bias=quarter[:])
+            nc.scalar.activation(ra[:], sq_sum[:], ACT.Sqrt, bias=quarter[:])
             if t == PACK - 1:
-                nc.scalar.copy(o_planes[:, t - 1, :], o_sb[t - 1][:])
+                nc.scalar.copy(o_tiles[:, t - 1, :], o_sb[t - 1][:])
             nc.vector.tensor_copy(o_sb[t][:].indirect(n3_t[:]), ra[:])
             if t < PACK - 2:
-                nc.sync.dma_start(o_planes[:, t, :], o_sb[t][:])
+                nc.sync.dma_start(o_tiles[:, t, :], o_sb[t][:])
             nc.sync.dma_start(out_rows[:, t, :], o_sb[t][:])
 
         for step in range(PACK + 1):
             if step < PACK:
                 pick_pairs(step)
             if step >= 1:
-                put_radius(step - 1)
+                put_roots(step - 1)
 
         o_scales = sb("o_scales", [P, S], U8)
         words_out = out_1[0].rearrange("p c r -> p (c r)").bitcast(I32)
         o_grouped = sb("o_grouped", [P, S * PACK], BF16)
-        for engine_copy, js in ((nc.vector.tensor_copy, slice(0, TAIL_SPLIT)), (nc.scalar.copy, slice(TAIL_SPLIT, S))):
-            engine_copy(o_planes[:, PACK - 1, js], o_sb[PACK - 1][:, js])
-            regroup(engine_copy, o_grouped[:, js.start * PACK : js.stop * PACK], o_planes[:, :, js])
+        for engine_copy, cuts in ((nc.vector.tensor_copy, (0, HALF, TAIL_SPLIT)), (nc.scalar.copy, (TAIL_SPLIT, S))):
+            for a, b in zip(cuts, cuts[1:]):
+                engine_copy(o_tiles[:, PACK - 1, a:b], o_sb[PACK - 1][:, a:b])
+            for a, b in zip(cuts, cuts[1:]):
+                regroup(engine_copy, o_grouped[:, a * PACK : b * PACK], o_tiles[:, :, a:b])
         for hf in range(2):
             js = slice(hf * HALF, (hf + 1) * HALF)
             o_words = sb("o_words%d" % hf, [P, HALF], U32)
@@ -277,6 +287,6 @@ def tile_picked_twqjointbpolar_none_po_kernel(
             )
             nc.sync.dma_start(words_out[:, js], o_words[:].bitcast(I32))
         scale_rows = out_2[0].bitcast(I32)
-        for q in range(4):
+        for q in range(QUADRANTS):
             queue = nc.scalar if q % 2 else nc.sync
             queue.dma_start(scale_rows[4 * q : 4 * q + 4, :], o_scales[32 * q : 32 * q + 4, :].bitcast(I32))

from contextlib import ExitStack

import concourse.mybir as mybir
from concourse.masks import make_identity

K, T, S, H, G, W = 512, 1024, 512, 512, 2048, 256
FLOPS = 3 * 2 * K * H * S

F32 = mybir.dt.float32
BF16 = mybir.dt.bfloat16
I32 = mybir.dt.int32
U32 = mybir.dt.uint32
U16 = mybir.dt.uint16
U8 = mybir.dt.uint8
FP8X4 = mybir.dt.float8_e4m3fn_x4
FP4X4 = mybir.dt.float4_e2m1fn_x4
ACT = mybir.ActivationFunctionType
ALU = mybir.AluOpType

P = 128
PACK = 4
QUADRANTS = 4
HALF = S // 2
UNITS = 2 * PACK
LAST_UNIT = UNITS - 1
H_SCALE = 0.0625

BOTH_ON_SCALAR = (0, 1, LAST_UNIT)
LAG = 2
N2_BUFS = 4
N1_BUFS = 2
EARLY_TILES = 2
TAIL_SPLIT = 320


def tile_picked_twqjointbpolar_none_po_kernel(
    tc, x_words, x_scales, w1_words, w1_scales, w2_words, w2_scales, gs, d_words, d_scales,
    offs, two, n1, n2, k1, n3, n4, out_0, out_1, out_2,
):
    nc = tc.nc
    with ExitStack() as ctx:
        keep = ctx.enter_context(tc.tile_pool(name="keep", bufs=1))
        psum = ctx.enter_context(tc.psum_pool(name="psum", bufs=1))

        def sb(name, shape, dtype, tag=None, bufs=1):
            return keep.tile(shape, dtype, name=name, tag=tag or name, bufs=bufs, align_bytes=64)

        def load_list(name, src):
            tile = keep.tile(list(src.shape), U16, name=name)
            nc.sync.dma_start(tile[:], src)
            return tile

        def load_scale_rows(queues, tile, src, repeats):
            rows = src[0].bitcast(I32)
            for q, queue in enumerate(queues):
                four = rows[4 * q : 4 * q + 4, :]
                queue.dma_start(
                    tile[32 * q : 32 * q + 4 * repeats, :].bitcast(I32),
                    four.partition_broadcast(repeats) if repeats > 1 else four,
                )

        def entries(lst, start, count):
            return lst[:, start // 16 : (start + count) // 16]

        def deal(engine_copy, dealt, plain, walk="p m t"):
            engine_copy(
                out=dealt.rearrange("p (t m) -> " + walk, t=PACK), in_=plain.rearrange("p (m t) -> " + walk, t=PACK)
            )

        def regroup(engine_copy, grouped, tiles):
            engine_copy(
                out=grouped.rearrange("p (c i t) -> p c t i", i=4, t=PACK),
                in_=tiles.rearrange("p t (c i) -> p c t i", i=4),
            )

        def pieces(width):
            return [slice(c, c + width) for c in range(0, HALF, width)]

        x_tab = sb("x_tab", [P, T], U32)
        xs_tab = sb("xs_tab", [P, T], U8)
        w1_raw, w2_raw = (sb("w%d_raw" % i, [P, 2 * H], U8) for i in (1, 2))
        w1s_raw, w2s_raw = (sb("w%ds_raw" % i, [P, H], U8) for i in (1, 2))
        d_tab = sb("d_tab", [P, G], U32)
        ds_tab = sb("ds_tab", [P, G], U8)
        dk_scales = sb("dk_scales", [P, H], U8)
        gs_t = sb("gs_t", [P, PACK], F32)
        quarter = sb("quarter", [P, 1], F32)
        ident = sb("ident", [P, P], F32)

        nc.vector.memset(ds_tab[:].bitcast(I32), 0)
        nc.gpsimd.memset(w1s_raw[:].bitcast(I32), 0)
        load_scale_rows([nc.gpsimd] * QUADRANTS, w1s_raw, w1_scales, 1)
        nc.gpsimd.memset(dk_scales[:].bitcast(I32), 0)
        nc.gpsimd.memset(quarter[:], 0.25)
        make_identity(nc, ident[:])

        two_t = load_list("two_t", two)
        load_scale_rows([nc.sync] * 2 + [nc.scalar] * 2, xs_tab, x_scales, 8)
        nc.sync.dma_start(x_tab[:].bitcast(I32), x_words[0].rearrange("p c r -> p (c r)").bitcast(I32))
        nc.sync.dma_start(w2_raw[:].bitcast(I32), w2_words[0].bitcast(I32))
        load_scale_rows([nc.sync] * QUADRANTS, w2s_raw, w2_scales, 8)
        nc.sync.dma_start(w1_raw[:].bitcast(I32), w1_words[0].bitcast(I32))
        offs_t = load_list("offs_t", offs)
        n2_t = load_list("n2_t", n2)
        n1_t = load_list("n1_t", n1)
        nc.sync.dma_start(d_tab[:].bitcast(I32), d_words[0].rearrange("p c r -> p (c r)").bitcast(I32))
        nc.sync.dma_start(ds_tab[0:P:8, :].bitcast(I32), d_scales[0].bitcast(I32))
        k1_t = load_list("k1_t", k1)
        nc.sync.dma_start(gs_t[:], gs.rearrange("(p t) o -> p (t o)", t=PACK))
        n3_t = load_list("n3_t", n3)
        n4_t = load_list("n4_t", n4)

        def token_product(name, w_raw, ws_raw, deal_scales, lst, bank_tag):
            w_dealt = sb(name + "_w", [P, 2 * H], U8)
            ws_dealt = sb(name + "_ws", [P, H], U8)
            deal(nc.scalar.copy, w_dealt[:].bitcast(U16), w_raw[:].bitcast(U16))
            deal_scales(ws_dealt[:], ws_raw[:])
            x_picked = sb(name + "_x", [P, S], U32)
            xs_picked = sb(name + "_xs", [P, S], U8)
            nc.vector.tensor_copy(xs_picked[:], xs_tab[:].indirect(lst[:]))
            nc.vector.tensor_copy(x_picked[:], x_tab[:].indirect(lst[:]))
            banks = []
            for t in range(PACK):
                bank = psum.tile([P, S], F32, name="%s_ps%d" % (name, t), tag="%s%d" % (bank_tag, t))
                nc.tensor.matmul_mx(
                    out=bank[:],
                    lhsT=w_dealt[:, 2 * P * t : 2 * P * (t + 1)].bitcast(FP4X4),
                    lhsT_scale=ws_dealt[:, P * t : P * (t + 1)],
                    rhs=x_picked[:].bitcast(FP8X4),
                    rhs_scale=xs_picked[:],
                    start=True,
                    stop=True,
                )
                banks.append(bank)
            return banks

        d_ps = token_product(
            "d", w2_raw, w2s_raw, lambda dealt, plain: deal(nc.vector.tensor_copy, dealt, plain), two_t, "low"
        )
        d_sb = [sb("d_sb%d" % t, [P, S], F32) for t in range(PACK)]
        y_ps = token_product(
            "y", w1_raw, w1s_raw, lambda dealt, plain: deal(nc.gpsimd.tensor_copy, dealt, plain, "p t m"), offs_t, "high"
        )

        dk_picked = sb("dk_picked", [P, H], U32)
        dks_picked = sb("dks_picked", [P, H], U8)
        dk_words = sb("dk_words", [P, H], U32)
        dks_dealt = sb("dks_dealt", [P, H], U8)
        nc.vector.tensor_copy(dks_picked[:], ds_tab[:].indirect(k1_t[:]))
        deal(nc.vector.tensor_copy, dks_dealt[:], dks_picked[:])
        for r in range(4):
            nc.sync.dma_start(dk_scales[r:P:32, :].bitcast(I32), dks_dealt[8 * r : P : 32, :].bitcast(I32))
        nc.vector.tensor_copy(dk_picked[:], d_tab[:].indirect(k1_t[:]))
        deal(nc.vector.tensor_copy, dk_words[:], dk_picked[:])

        h_ps = [psum.tile([P, S], F32, name="h_ps%d" % t, tag="low%d" % t) for t in range(PACK)]
        h_sb = [sb("h_sb%d" % t, [P, S], F32) for t in range(PACK)]
        z_tiles = [sb("z_tiles%d" % hf, [P, PACK, HALF], BF16) for hf in range(2)]
        diffs = sb("diffs", [P, UNITS, HALF], F32, tag="dk_picked")

        def look_up_d(u):
            hf, t = divmod(u, PACK)
            if hf == 0:
                nc.scalar.activation(d_sb[t][:], d_ps[t][:], ACT.Copy)
            at_n2 = sb("at_n2_%d" % u, [P, HALF], F32, tag="at_n2", bufs=N2_BUFS)
            nc.scalar.activation(at_n2[:], d_sb[t][:].indirect(entries(n2_t, hf * HALF, HALF)), ACT.Copy)
            window_n1 = d_sb[t][:].indirect(entries(n1_t, hf * HALF, HALF))
            if u in BOTH_ON_SCALAR:
                at_n1 = sb("at_n1_%d" % u, [P, HALF], F32, tag="at_n1", bufs=N1_BUFS)
                nc.scalar.activation(at_n1[:], window_n1, ACT.Copy)
                nc.vector.tensor_tensor(diffs[:, u, :], at_n1[:], at_n2[:], ALU.subtract)
            else:
                nc.vector.tensor_tensor(diffs[:, u, :], window_n1, at_n2[:], ALU.subtract)

        def gate(u):
            hf, t = divmod(u, PACK)
            th = sb("th%d" % u, [P, HALF], F32)
            nc.scalar.activation(th[:], diffs[:, u, :], ACT.Tanh)
            if u == LAST_UNIT:
                warm = sb("warm", [P, 1], F32)
                nc.scalar.activation(warm[:], th[:, 0:1], ACT.Sqrt, bias=quarter[:], scale=0.0)
            y_half = y_ps[t][:, hf * HALF : (hf + 1) * HALF]
            for js in pieces(HALF // 2 if u == LAST_UNIT else HALF):
                nc.vector.scalar_tensor_tensor(
                    out=z_tiles[hf][:, t, js], in0=y_half[:, js], scalar=gs_t[:, t : t + 1], in1=th[:, js],
                    op0=ALU.mult, op1=ALU.mult,
                )

        def coded_product(hf):
            z_grouped = sb("z_grouped%d" % hf, [P, HALF * PACK], BF16)
            z_words = sb("z_words%d" % hf, [P, HALF], U32)
            z_scales = sb("z_scales%d" % hf, [P, HALF], U8)
            cut = pieces(HALF // 2 if hf == 1 else HALF)
            for js in cut:
                regroup(nc.vector.tensor_copy, z_grouped[:, js.start * PACK : js.stop * PACK], z_tiles[hf][:, :, js])
            for js in cut:
                nc.vector.quantize_mx(
                    out=z_words[:, js].bitcast(FP8X4), scales=z_scales[:, js],
                    in_=z_grouped[:, js.start * PACK : js.stop * PACK],
                )
            for t in range(PACK):
                for js in cut if t == 0 else pieces(HALF):
                    nc.tensor.matmul_mx(
                        out=h_ps[t][:, hf * HALF + js.start : hf * HALF + js.stop],
                        lhsT=dk_words[:, P * t : P * (t + 1)].bitcast(FP8X4),
                        lhsT_scale=dk_scales[:, P * t : P * (t + 1)],
                        rhs=z_words[:, js].bitcast(FP8X4),
                        rhs_scale=z_scales[:, js],
                        start=True,
                        stop=True,
                    )

        def h_out_of_psum(t, js):
            nc.scalar.activation(h_sb[t][:, js], h_ps[t][:, js], ACT.Copy, scale=H_SCALE)

        for step in range(UNITS + LAG):
            if step < UNITS:
                look_up_d(step)
            if step == UNITS:
                for t in range(EARLY_TILES):
                    h_out_of_psum(t, slice(0, HALF))
            if step >= LAG:
                gate(step - LAG)
                if (step - LAG) % PACK == PACK - 1:
                    coded_product((step - LAG) // PACK)

        out_rows = out_0.rearrange("(p t) c -> p t c", t=PACK)
        o_tiles = sb("o_tiles", [P, PACK, S], F32)
        o_sb = [sb("o_sb%d" % t, [P, S], F32) for t in range(PACK)]
        turned = {}

        def pick_pairs(t):
            if t == 0:
                nc.vector.tensor_scalar(h_sb[t][:, HALF:], h_ps[t][:, HALF:], H_SCALE, None, ALU.mult)
            else:
                h_out_of_psum(t, slice(HALF if t < EARLY_TILES else 0, S))
            pair = sb("pair%d" % t, [P, 2 * W], F32)
            nc.scalar.activation(pair[:, :W], h_sb[t][:].indirect(n3_t[:]), ACT.Copy, scale=-0.5)
            if t == 0:
                nc.vector.tensor_copy(pair[:, W:], h_sb[t][:].indirect(n4_t[:]))
            else:
                nc.scalar.activation(pair[:, W:], h_sb[t][:].indirect(n4_t[:]), ACT.Copy)
            nc.vector.tensor_tensor(o_sb[t][:].indirect(n4_t[:]), pair[:, :W], pair[:, W:], ALU.add)
            turned[t] = psum.tile([P, 2 * W], F32, name="turned%d" % t, tag="high%d" % (t % 2))
            for b in range(2 * W // P):
                nc.tensor.transpose(turned[t][:, b * P : (b + 1) * P], pair[:, b * P : (b + 1) * P], ident[:])

        def put_roots(t):
            sq = o_tiles[:, PACK - 2, :] if t == PACK - 1 else sb("sq%d" % t, [P, 2 * W], F32)
            ra = sb("ra%d" % t, [P, W], F32)
            nc.scalar.activation(sq[:, :W], turned[t][:, :W], ACT.Square, scale=2.0)
            nc.scalar.activation(sq[:, W:], turned[t][:, W:], ACT.Square)
            sq_sum = psum.tile([P, W], F32, name="sq_sum%d" % t, tag="high%d" % (2 + t % 2))
            for b in range(W // P):
                for side in range(2):
                    nc.tensor.matmul(
                        sq_sum[:, b * P : (b + 1) * P], sq[:, side * W + b * P : side * W + (b + 1) * P], ident[:],
                        start=side == 0, stop=side == 1, is_transpose=True,
                    )
            nc.scalar.activation(ra[:], sq_sum[:], ACT.Sqrt, bias=quarter[:])
            if t == PACK - 1:
                nc.scalar.copy(o_tiles[:, t - 1, :], o_sb[t - 1][:])
            nc.vector.tensor_copy(o_sb[t][:].indirect(n3_t[:]), ra[:])
            if t < PACK - 2:
                nc.sync.dma_start(o_tiles[:, t, :], o_sb[t][:])
            nc.sync.dma_start(out_rows[:, t, :], o_sb[t][:])

        for step in range(PACK + 1):
            if step < PACK:
                pick_pairs(step)
            if step >= 1:
                put_roots(step - 1)

        o_scales = sb("o_scales", [P, S], U8)
        words_out = out_1[0].rearrange("p c r -> p (c r)").bitcast(I32)
        o_grouped = sb("o_grouped", [P, S * PACK], BF16)
        for engine_copy, cuts in ((nc.vector.tensor_copy, (0, HALF, TAIL_SPLIT)), (nc.scalar.copy, (TAIL_SPLIT, S))):
            for a, b in zip(cuts, cuts[1:]):
                engine_copy(o_tiles[:, PACK - 1, a:b], o_sb[PACK - 1][:, a:b])
            for a, b in zip(cuts, cuts[1:]):
                regroup(engine_copy, o_grouped[:, a * PACK : b * PACK], o_tiles[:, :, a:b])
        for hf in range(2):
            js = slice(hf * HALF, (hf + 1) * HALF)
            o_words = sb("o_words%d" % hf, [P, HALF], U32)
            nc.vector.quantize_mx(
                out=o_words[:].bitcast(FP8X4), scales=o_scales[:, js], in_=o_grouped[:, js.start * PACK : js.stop * PACK]
            )
            nc.sync.dma_start(words_out[:, js], o_words[:].bitcast(I32))
        scale_rows = out_2[0].bitcast(I32)
        for q in range(QUADRANTS):
            queue = nc.scalar if q % 2 else nc.sync
            queue.dma_start(scale_rows[4 * q : 4 * q + 4, :], o_scales[32 * q : 32 * q + 4, :].bitcast(I32))
